import numpy as np, ml_dtypes
CORES = [3,5,19,21,35,37,51,53,67,69]
N = 10
TK = 256
COEF = [[-2,1,1,-2,2,1,-1,2,-1,2],[2,-2,1,1,2,1,3,1,2,2],[1,-2,-2,1,2,2,1,2,1,-2],[-1,2,1,-1,2,3,-1,1,1,3],[-2,2,3,1,2,-1,-1,-1,3,3],[-1,3,-2,-2,1,-1,3,1,-1,1],[3,1,1,3,3,3,-1,3,-2,-1],[2,-2,3,1,-2,1,3,3,-2,2],[-2,3,-1,2,2,-1,2,3,1,-1],[1,1,2,-1,2,-1,-1,-2,-2,-2]]
def setup_inputs(rng):
    return {"x": rng.standard_normal((N, 128, TK), dtype=np.float32).astype(ml_dtypes.bfloat16), "a": (rng.standard_normal((N, 128, 128), dtype=np.float32) / 11).astype(ml_dtypes.bfloat16)}
def setup_inputs_big(rng):
    d = setup_inputs(rng)
    for k in ("x", "a"): d[k] = (d[k].astype(np.float32) * 1024.0).astype(d[k].dtype)
    return d
def setup_inputs_small(rng):
    d = setup_inputs(rng)
    for k in ("x", "a"): d[k] = (d[k].astype(np.float32) * (1 / 1024.0)).astype(d[k].dtype)
    return d
def setup_inputs_apart(rng):
    d = setup_inputs(rng)
    f = (10.0 ** rng.permutation(np.linspace(-1.5, 1.5, N))).astype(np.float32).reshape(N, 1, 1)
    for k in ("x", "a"): d[k] = (d[k].astype(np.float32) * f).astype(d[k].dtype)
    return d
def reference(x, a):
    X, A = x.astype(np.float64), a.astype(np.float64)
    y = np.stack([A[r].T @ sum(COEF[r][j] * X[j] for j in range(N)) for r in range(N)])
    return {"y": y.astype(ml_dtypes.bfloat16)}

@@ -1,0 +1,128 @@
+from concourse.bass import DstId, RemoteDMATransfer
+from concourse.mybir import AluOpType
+
+TK = 256
+M = 128
+NCH = 5
+NCONST = 4
+
+SCRATCH = {
+    "xall": ("sbuf", [128, NCH * TK], "bfloat16"),
+    "a_own": ("sbuf", [128, M], "bfloat16"),
+    "a_par": ("sbuf", [128, M], "bfloat16"),
+    "s_own": ("sbuf", [128, NCONST * M], "bfloat16"),
+    "s_par": ("sbuf", [128, NCONST * M], "bfloat16"),
+    "y_send": ("sbuf", [128, TK], "bfloat16"),
+    "y_land": ("sbuf", [128, TK], "bfloat16"),
+    "y_out": ("sbuf", [128, TK], "bfloat16"),
+    "cst": ("psum", [128, 512], "float32"),
+    "p_own": ("psum", [128, 512], "float32"),
+    "p_par": ("psum", [128, 512], "float32"),
+}
+SEMAPHORES = ["x_ld", "a_ld", "filled", "scaled", "a_arr", "par_done", "own_done", "rounded", "y_arr", "summed",
+              "stored", "sent"] + ["arr%d" % k for k in range(NCH)]
+
+
+def _bits(mask):
+    return bin(mask).count("1")
+
+
+def rank_program(g, core, T, topo):
+    rank = T.rank_of(core)
+    if rank is None:
+        return
+    coef = T.tables["COEF"]
+    sem = T.sem
+
+    chips = sorted({topo.chip(c) for c in T.cores})
+    me = chips.index(topo.chip(core))
+    partner = [c for c in T.cores if c != core and topo.chip(c) == topo.chip(core)][0]
+    prank = T.rank_of(partner)
+    same_die = [[c for c in T.cores if topo.chip(c) == ch and topo.die(c) == topo.die(core)][0] for ch in chips]
+    out_order = [(me + o) % len(chips) for o in range(1, len(chips))]
+    in_order = [(me - o) % len(chips) for o in range(1, len(chips))]
+
+    def slot(k):
+        return T.xall[:, k * TK:(k + 1) * TK]
+
+    off_mask = topo.mask(core, same_die[out_order[0]])
+    chip_mask = topo.mask(core, partner)
+    rest_mask = chip_mask & ~off_mask
+
+    consts = sorted({c for row in coef for c in row} - {0, 1})
+    need_own = [c for c in consts if c in {coef[rank][T.rank_of(s)] for s in same_die}]
+    need_par = [c for c in consts if c in {coef[prank][T.rank_of(s)] for s in same_die}]
+    need_any = [c for c in consts if c in need_own or c in need_par]
+
+    def block(t, c):
+        i = consts.index(c)
+        return t[:, i * M:(i + 1) * M]
+
+    g.sync.dma_start(slot(me), T.x[:]).then_inc(sem.x_ld, 16)
+    g.scalar.dma_start(T.a_own[:], T.a[:]).then_inc(sem.a_ld, 16)
+
+    g.wait_ge(sem.x_ld, 16)
+    ids = []
+    for k in out_order:
+        rid, pid, _ = topo.addr(same_die[k])
+        ids.append(DstId(rid=rid, pnc=pid))
+    g.remote_dma_fused(
+        [RemoteDMATransfer(dst_ids=ids, dma_engine_mask=off_mask, remote_sem=sem["arr%d" % me],
+                           srcs=[slot(me)], dsts=[slot(me) for _ in out_order], alu_op=0)],
+        local_sem=sem.sent)
+    prid, ppid, _ = topo.addr(partner)
+    g.wait_ge(sem.a_ld, 16)
+    g.remote_dma(out_ap=T.a_par[:], in_ap=T.a_own[:], remote_sem=sem.a_arr, local_sem=sem.sent,
+                 pid=ppid, routing_id=prid, dma_engine_mask=rest_mask)
+    g.wait_ge(sem.rounded, 1)
+    g.remote_dma(out_ap=T.y_land[:], in_ap=T.y_send[:], remote_sem=sem.y_arr, local_sem=sem.sent,
+                 pid=ppid, routing_id=prid, dma_engine_mask=chip_mask)
+    g.wait_ge(sem.sent, _bits(off_mask) + _bits(rest_mask) + _bits(chip_mask))
+
+    v = g.vector
+    for c in need_any:
+        v.memset(block(T.cst, c), float(c)).then_inc(sem.filled, 1)
+    v.wait_ge(sem.filled, len(need_any))
+    v.wait_ge(sem.a_ld, 16)
+    for c in need_own:
+        v.tensor_tensor(block(T.s_own, c), T.a_own[:], block(T.cst, c), AluOpType.mult).then_inc(sem.scaled, 1)
+    v.wait_ge(sem.a_arr, _bits(rest_mask))
+    for c in need_par:
+        v.tensor_tensor(block(T.s_par, c), T.a_par[:], block(T.cst, c), AluOpType.mult).then_inc(sem.scaled, 1)
+    v.wait_ge(sem.par_done, 1)
+    v.tensor_copy(T.y_send[:], T.p_par[:, 0:TK]).then_inc(sem.rounded, 1)
+    v.wait_ge(sem.own_done, 1)
+    v.wait_ge(sem.y_arr, _bits(chip_mask))
+    v.tensor_tensor(T.y_out[:], T.p_own[:, 0:TK], T.y_land[:], AluOpType.add).then_inc(sem.summed, 1)
+
+    t = g.tensor
+    t.wait_ge(sem.x_ld, 16)
+    t.wait_ge(sem.a_ld, 16)
+    t.wait_ge(sem.a_arr, _bits(rest_mask))
+    t.wait_ge(sem.scaled, len(need_own) + len(need_par))
+    order = [me] + in_order
+    jobs = []
+    for k in order:
+        j = T.rank_of(same_die[k])
+        for r, raw, scaled, acc, done in ((prank, T.a_par, T.s_par, T.p_par, sem.par_done),
+                                          (rank, T.a_own, T.s_own, T.p_own, sem.own_done)):
+            c = coef[r][j]
+            if c != 0:
+                jobs.append((k, r, raw[:] if c == 1 else block(scaled, c), acc, done))
+    waited = {me}
+    for n, (k, r, lhsT, acc, done) in enumerate(jobs):
+        if k not in waited:
+            t.wait_ge(sem["arr%d" % k], _bits(off_mask))
+            waited.add(k)
+        first = not any(q[1] == r for q in jobs[:n])
+        last = not any(q[1] == r for q in jobs[n + 1:])
+        mm = t.matmul(acc[:, 0:TK], lhsT, slot(k), start=first, stop=last)
+        if last:
+            mm.then_inc(done, 1)
+    for k in in_order:
+        if k not in waited:
+            t.wait_ge(sem["arr%d" % k], _bits(off_mask))
+
+    g.sync.wait_ge(sem.summed, 1)
+    g.sync.dma_start(T.y[:], T.y_out[:]).then_inc(sem.stored, 16)
+    g.sync.wait_ge(sem.stored, 16)

@@ -3,11 +3,13 @@ from concourse.mybir import AluOpType
 
 TK = 256
 M = 128
+N = 10
 NCH = 5
 NCONST = 4
 
 SCRATCH = {
     "xall": ("sbuf", [128, NCH * TK], "bfloat16"),
+    "xcross": ("sbuf", [128, TK], "bfloat16"),
     "a_own": ("sbuf", [128, M], "bfloat16"),
     "a_par": ("sbuf", [128, M], "bfloat16"),
     "s_own": ("sbuf", [128, NCONST * M], "bfloat16"),
@@ -19,8 +21,8 @@ SCRATCH = {
     "p_own": ("psum", [128, 512], "float32"),
     "p_par": ("psum", [128, 512], "float32"),
 }
-SEMAPHORES = ["x_ld", "a_ld", "filled", "scaled", "a_arr", "par_done", "own_done", "rounded", "y_arr", "summed",
-              "stored", "sent"] + ["arr%d" % k for k in range(NCH)]
+SEMAPHORES = (["x_ld", "a_ld", "filled", "scaled_own", "a_arr", "par_done", "own_done", "rounded", "y_arr", "summed",
+               "stored", "sent"] + ["arr%d" % r for r in range(N)] + ["scaled_par%d" % i for i in range(NCONST)])
 
 
 def _bits(mask):
@@ -35,23 +37,37 @@ def rank_program(g, core, T, topo):
     sem = T.sem
 
     chips = sorted({topo.chip(c) for c in T.cores})
+    nch = len(chips)
     me = chips.index(topo.chip(core))
     partner = [c for c in T.cores if c != core and topo.chip(c) == topo.chip(core)][0]
     prank = T.rank_of(partner)
     same_die = [[c for c in T.cores if topo.chip(c) == ch and topo.die(c) == topo.die(core)][0] for ch in chips]
-    out_order = [(me + o) % len(chips) for o in range(1, len(chips))]
-    in_order = [(me - o) % len(chips) for o in range(1, len(chips))]
+    other_die = [[c for c in T.cores if topo.chip(c) == ch and topo.die(c) != topo.die(core)][0] for ch in chips]
+    out_order = [(me + o) % nch for o in range(1, nch)]
+    in_order = [(me - o) % nch for o in range(1, nch)]
+    early, late = in_order[:-1], in_order[-1]
 
     def slot(k):
         return T.xall[:, k * TK:(k + 1) * TK]
 
     off_mask = topo.mask(core, same_die[out_order[0]])
-    chip_mask = topo.mask(core, partner)
-    rest_mask = chip_mask & ~off_mask
+    rest_mask = topo.mask(core, partner) & ~off_mask
+    n_off, n_rest = _bits(off_mask), _bits(rest_mask)
+
+    def job(k, r):
+        return (slot(k), T.rank_of(same_die[k]), r)
+
+    jobs = ([job(me, rank), job(early[0], rank)]
+            + [job(k, prank) for k in [me] + early]
+            + [job(k, rank) for k in early[1:] + [late]]
+            + [(T.xcross[:], T.rank_of(other_die[late]), rank)])
 
     consts = sorted({c for row in coef for c in row} - {0, 1})
-    need_own = [c for c in consts if c in {coef[rank][T.rank_of(s)] for s in same_die}]
-    need_par = [c for c in consts if c in {coef[prank][T.rank_of(s)] for s in same_die}]
+    need_own = [c for c in consts if c in {coef[r][j] for _, j, r in jobs if r == rank}]
+    need_par = []
+    for _, j, r in jobs:
+        if r == prank and coef[r][j] in consts and coef[r][j] not in need_par:
+            need_par.append(coef[r][j])
     need_any = [c for c in consts if c in need_own or c in need_par]
 
     def block(t, c):
@@ -62,13 +78,15 @@ def rank_program(g, core, T, topo):
     g.scalar.dma_start(T.a_own[:], T.a[:]).then_inc(sem.a_ld, 16)
 
     g.wait_ge(sem.x_ld, 16)
+    dst_cores = [same_die[k] for k in out_order] + [other_die[out_order[-1]]]
+    dst_aps = [slot(me) for _ in out_order] + [T.xcross[:]]
     ids = []
-    for k in out_order:
-        rid, pid, _ = topo.addr(same_die[k])
+    for c in dst_cores:
+        rid, pid, _ = topo.addr(c)
         ids.append(DstId(rid=rid, pnc=pid))
     g.remote_dma_fused(
-        [RemoteDMATransfer(dst_ids=ids, dma_engine_mask=off_mask, remote_sem=sem["arr%d" % me],
-                           srcs=[slot(me)], dsts=[slot(me) for _ in out_order], alu_op=0)],
+        [RemoteDMATransfer(dst_ids=ids, dma_engine_mask=off_mask, remote_sem=sem["arr%d" % rank],
+                           srcs=[slot(me)], dsts=dst_aps, alu_op=0)],
         local_sem=sem.sent)
     prid, ppid, _ = topo.addr(partner)
     g.wait_ge(sem.a_ld, 16)
@@ -76,8 +94,8 @@ def rank_program(g, core, T, topo):
                  pid=ppid, routing_id=prid, dma_engine_mask=rest_mask)
     g.wait_ge(sem.rounded, 1)
     g.remote_dma(out_ap=T.y_land[:], in_ap=T.y_send[:], remote_sem=sem.y_arr, local_sem=sem.sent,
-                 pid=ppid, routing_id=prid, dma_engine_mask=chip_mask)
-    g.wait_ge(sem.sent, _bits(off_mask) + _bits(rest_mask) + _bits(chip_mask))
+                 pid=ppid, routing_id=prid, dma_engine_mask=rest_mask)
+    g.wait_ge(sem.sent, n_off + 2 * n_rest)
 
     v = g.vector
     for c in need_any:
@@ -85,43 +103,43 @@ def rank_program(g, core, T, topo):
     v.wait_ge(sem.filled, len(need_any))
     v.wait_ge(sem.a_ld, 16)
     for c in need_own:
-        v.tensor_tensor(block(T.s_own, c), T.a_own[:], block(T.cst, c), AluOpType.mult).then_inc(sem.scaled, 1)
-    v.wait_ge(sem.a_arr, _bits(rest_mask))
+        v.tensor_tensor(block(T.s_own, c), T.a_own[:], block(T.cst, c), AluOpType.mult).then_inc(sem.scaled_own, 1)
+    v.wait_ge(sem.a_arr, n_rest)
     for c in need_par:
-        v.tensor_tensor(block(T.s_par, c), T.a_par[:], block(T.cst, c), AluOpType.mult).then_inc(sem.scaled, 1)
+        v.tensor_tensor(block(T.s_par, c), T.a_par[:], block(T.cst, c),
+                        AluOpType.mult).then_inc(sem["scaled_par%d" % consts.index(c)], 1)
     v.wait_ge(sem.par_done, 1)
     v.tensor_copy(T.y_send[:], T.p_par[:, 0:TK]).then_inc(sem.rounded, 1)
     v.wait_ge(sem.own_done, 1)
-    v.wait_ge(sem.y_arr, _bits(chip_mask))
+    v.wait_ge(sem.y_arr, n_rest)
     v.tensor_tensor(T.y_out[:], T.p_own[:, 0:TK], T.y_land[:], AluOpType.add).then_inc(sem.summed, 1)
 
     t = g.tensor
     t.wait_ge(sem.x_ld, 16)
     t.wait_ge(sem.a_ld, 16)
-    t.wait_ge(sem.a_arr, _bits(rest_mask))
-    t.wait_ge(sem.scaled, len(need_own) + len(need_par))
-    order = [me] + in_order
-    jobs = []
-    for k in order:
-        j = T.rank_of(same_die[k])
-        for r, raw, scaled, acc, done in ((prank, T.a_par, T.s_par, T.p_par, sem.par_done),
-                                          (rank, T.a_own, T.s_own, T.p_own, sem.own_done)):
-            c = coef[r][j]
-            if c != 0:
-                jobs.append((k, r, raw[:] if c == 1 else block(scaled, c), acc, done))
-    waited = {me}
-    for n, (k, r, lhsT, acc, done) in enumerate(jobs):
-        if k not in waited:
-            t.wait_ge(sem["arr%d" % k], _bits(off_mask))
-            waited.add(k)
-        first = not any(q[1] == r for q in jobs[:n])
-        last = not any(q[1] == r for q in jobs[n + 1:])
-        mm = t.matmul(acc[:, 0:TK], lhsT, slot(k), start=first, stop=last)
-        if last:
+    t.wait_ge(sem.scaled_own, len(need_own))
+    live = [n for n, (_, j, r) in enumerate(jobs) if coef[r][j] != 0]
+    seen = {rank}
+    for n, (x_ap, j, r) in enumerate(jobs):
+        if j not in seen:
+            t.wait_ge(sem["arr%d" % j], n_off)
+            seen.add(j)
+        if r == prank and "a_par" not in seen:
+            t.wait_ge(sem.a_arr, n_rest)
+            seen.add("a_par")
+        if n not in live:
+            continue
+        c = coef[r][j]
+        if r == prank and c != 1 and ("par", c) not in seen:
+            t.wait_ge(sem["scaled_par%d" % consts.index(c)], 1)
+            seen.add(("par", c))
+        raw, scaled, acc, done = ((T.a_own, T.s_own, T.p_own, sem.own_done) if r == rank
+                                  else (T.a_par, T.s_par, T.p_par, sem.par_done))
+        group = [q for q in live if jobs[q][2] == r]
+        mm = t.matmul(acc[:, 0:TK], raw[:] if c == 1 else block(scaled, c), x_ap,
+                      start=(n == group[0]), stop=(n == group[-1]))
+        if n == group[-1]:
             mm.then_inc(done, 1)
-    for k in in_order:
-        if k not in waited:
-            t.wait_ge(sem["arr%d" % k], _bits(off_mask))
 
     g.sync.wait_ge(sem.summed, 1)
     g.sync.dma_start(T.y[:], T.y_out[:]).then_inc(sem.stored, 16)

@@ -1,15 +1,23 @@
 from concourse.bass import DstId, RemoteDMATransfer
-from concourse.mybir import AluOpType
+from concourse.mybir import AluOpType, ActivationFunctionType
 
 TK = 256
 M = 128
 N = 10
-NCH = 5
 NCONST = 4
+NRAW = 2
+NB = 4
+NH = 2
 
 SCRATCH = {
-    "xall": ("sbuf", [128, NCH * TK], "bfloat16"),
-    "xcross": ("sbuf", [128, TK], "bfloat16"),
+    "x_own": ("sbuf", [128, TK], "bfloat16"),
+    "x_par": ("sbuf", [128, TK], "bfloat16"),
+    "raw0": ("sbuf", [128, TK], "bfloat16"),
+    "raw1": ("sbuf", [128, TK], "bfloat16"),
+    "mixin0": ("sbuf", [128, TK], "bfloat16"),
+    "mixin1": ("sbuf", [128, TK], "bfloat16"),
+    "mixout0": ("sbuf", [128, TK], "bfloat16"),
+    "mixout1": ("sbuf", [128, TK], "bfloat16"),
     "a_own": ("sbuf", [128, M], "bfloat16"),
     "a_par": ("sbuf", [128, M], "bfloat16"),
     "s_own": ("sbuf", [128, NCONST * M], "bfloat16"),
@@ -17,12 +25,17 @@ SCRATCH = {
     "y_send": ("sbuf", [128, TK], "bfloat16"),
     "y_land": ("sbuf", [128, TK], "bfloat16"),
     "y_out": ("sbuf", [128, TK], "bfloat16"),
-    "cst": ("psum", [128, 512], "float32"),
-    "p_own": ("psum", [128, 512], "float32"),
-    "p_par": ("psum", [128, 512], "float32"),
+    "tmp": ("psum", [128, 512], "float32"),
 }
-SEMAPHORES = (["x_ld", "a_ld", "filled", "scaled_own", "a_arr", "par_done", "own_done", "rounded", "y_arr", "summed",
-               "stored", "sent"] + ["arr%d" % r for r in range(N)] + ["scaled_par%d" % i for i in range(NCONST)])
+for _b in range(NB):
+    SCRATCH["p_own%d" % _b] = ("psum", [128, 512], "float32")
+for _h in range(NH):
+    SCRATCH["p_par%d" % _h] = ("psum", [128, 512], "float32")
+
+SEMAPHORES = (["x_ld", "a_ld", "scaled_own", "xs_arr", "a_arr", "tmp_done", "mixed0", "mixed1", "rounded", "y_arr",
+               "summed", "stored", "sent"]
+              + ["arr%d" % r for r in range(N)] + ["scaled_par%d" % i for i in range(NCONST)]
+              + ["own_done%d" % b for b in range(NB)] + ["par_done%d" % h for h in range(NH)])
 
 
 def _bits(mask):
@@ -45,102 +58,142 @@ def rank_program(g, core, T, topo):
     other_die = [[c for c in T.cores if topo.chip(c) == ch and topo.die(c) != topo.die(core)][0] for ch in chips]
     out_order = [(me + o) % nch for o in range(1, nch)]
     in_order = [(me - o) % nch for o in range(1, nch)]
-    early, late = in_order[:-1], in_order[-1]
-
-    def slot(k):
-        return T.xall[:, k * TK:(k + 1) * TK]
+    out_raw, out_mix = out_order[:NRAW], out_order[NRAW:]
+    in_raw, in_mix = in_order[:NRAW], in_order[NRAW:]
+    raw_land = [T.raw0, T.raw1]
+    mix_land = [T.mixin0, T.mixin1]
+    mix_out = [T.mixout0, T.mixout1]
 
     off_mask = topo.mask(core, same_die[out_order[0]])
     rest_mask = topo.mask(core, partner) & ~off_mask
     n_off, n_rest = _bits(off_mask), _bits(rest_mask)
 
-    def job(k, r):
-        return (slot(k), T.rank_of(same_die[k]), r)
+    def mix_rule(r, s_me, s_par):
+        cm, cp = coef[r][s_me], coef[r][s_par]
+        if cp != 0:
+            return cm / cp, True, cp
+        return 1.0, False, cm
 
-    jobs = ([job(me, rank), job(early[0], rank)]
-            + [job(k, prank) for k in [me] + early]
-            + [job(k, rank) for k in early[1:] + [late]]
-            + [(T.xcross[:], T.rank_of(other_die[late]), rank)])
+    def src(k):
+        return T.rank_of(same_die[k])
+
+    def arr(k):
+        return ("arr%d" % src(k), n_off)
+
+    jobs = [(T.x_own, None, coef[rank][rank], rank),
+            (T.x_par, ("xs_arr", n_rest), coef[rank][prank], rank),
+            (raw_land[0], arr(in_raw[0]), coef[rank][src(in_raw[0])], rank)]
+    jobs += [(raw_land[i], arr(k), coef[prank][src(k)], prank) for i, k in enumerate(in_raw)]
+    jobs += [(raw_land[i], arr(k), coef[rank][src(k)], rank) for i, k in enumerate(in_raw) if i > 0]
+    jobs += [(mix_land[i], arr(k), mix_rule(rank, src(k), T.rank_of(other_die[k]))[2], rank)
+             for i, k in enumerate(in_mix)]
 
     consts = sorted({c for row in coef for c in row} - {0, 1})
-    need_own = [c for c in consts if c in {coef[r][j] for _, j, r in jobs if r == rank}]
-    need_par = []
-    for _, j, r in jobs:
-        if r == prank and coef[r][j] in consts and coef[r][j] not in need_par:
-            need_par.append(coef[r][j])
-    need_any = [c for c in consts if c in need_own or c in need_par]
+    need_own, need_par = [], []
+    for _, _, w, r in jobs:
+        lst = need_own if r == rank else need_par
+        if w in consts and w not in lst:
+            lst.append(w)
 
     def block(t, c):
         i = consts.index(c)
         return t[:, i * M:(i + 1) * M]
 
-    g.sync.dma_start(slot(me), T.x[:]).then_inc(sem.x_ld, 16)
+    g.sync.dma_start(T.x_own[:], T.x[:]).then_inc(sem.x_ld, 16)
     g.scalar.dma_start(T.a_own[:], T.a[:]).then_inc(sem.a_ld, 16)
 
+    my_arr = sem["arr%d" % rank]
+    prid, ppid, _ = topo.addr(partner)
     g.wait_ge(sem.x_ld, 16)
-    dst_cores = [same_die[k] for k in out_order] + [other_die[out_order[-1]]]
-    dst_aps = [slot(me) for _ in out_order] + [T.xcross[:]]
     ids = []
-    for c in dst_cores:
-        rid, pid, _ = topo.addr(c)
+    for k in out_raw:
+        rid, pid, _ = topo.addr(same_die[k])
         ids.append(DstId(rid=rid, pnc=pid))
     g.remote_dma_fused(
-        [RemoteDMATransfer(dst_ids=ids, dma_engine_mask=off_mask, remote_sem=sem["arr%d" % rank],
-                           srcs=[slot(me)], dsts=dst_aps, alu_op=0)],
+        [RemoteDMATransfer(dst_ids=ids, dma_engine_mask=off_mask, remote_sem=my_arr,
+                           srcs=[T.x_own[:]], dsts=[raw_land[i][:] for i in range(len(out_raw))], alu_op=0)],
         local_sem=sem.sent)
-    prid, ppid, _ = topo.addr(partner)
+    g.remote_dma(out_ap=T.x_par[:], in_ap=T.x_own[:], remote_sem=sem.xs_arr, local_sem=sem.sent,
+                 pid=ppid, routing_id=prid, dma_engine_mask=rest_mask)
     g.wait_ge(sem.a_ld, 16)
     g.remote_dma(out_ap=T.a_par[:], in_ap=T.a_own[:], remote_sem=sem.a_arr, local_sem=sem.sent,
                  pid=ppid, routing_id=prid, dma_engine_mask=rest_mask)
-    g.wait_ge(sem.rounded, 1)
+    for i, k in enumerate(out_mix):
+        rid, pid, _ = topo.addr(same_die[k])
+        g.wait_ge(sem["mixed%d" % i], 1)
+        g.remote_dma(out_ap=mix_land[i][:], in_ap=mix_out[i][:], remote_sem=my_arr, local_sem=sem.sent,
+                     pid=pid, routing_id=rid, dma_engine_mask=off_mask)
+    g.wait_ge(sem.rounded, NH)
     g.remote_dma(out_ap=T.y_land[:], in_ap=T.y_send[:], remote_sem=sem.y_arr, local_sem=sem.sent,
                  pid=ppid, routing_id=prid, dma_engine_mask=rest_mask)
-    g.wait_ge(sem.sent, n_off + 2 * n_rest)
+    g.wait_ge(sem.sent, n_off * (1 + len(out_mix)) + 3 * n_rest)
+
+    sc = g.scalar
+    sc.wait_ge(sem.a_ld, 16)
+    for c in need_own:
+        sc.activation(block(T.s_own, c), T.a_own[:], ActivationFunctionType.Copy,
+                      scale=float(c)).then_inc(sem.scaled_own, 1)
+    sc.wait_ge(sem.a_arr, n_rest)
+    for i, c in enumerate(need_par):
+        sc.activation(block(T.s_par, c), T.a_par[:], ActivationFunctionType.Copy,
+                      scale=float(c)).then_inc(sem["scaled_par%d" % i], 1)
 
     v = g.vector
-    for c in need_any:
-        v.memset(block(T.cst, c), float(c)).then_inc(sem.filled, 1)
-    v.wait_ge(sem.filled, len(need_any))
-    v.wait_ge(sem.a_ld, 16)
-    for c in need_own:
-        v.tensor_tensor(block(T.s_own, c), T.a_own[:], block(T.cst, c), AluOpType.mult).then_inc(sem.scaled_own, 1)
-    v.wait_ge(sem.a_arr, n_rest)
-    for c in need_par:
-        v.tensor_tensor(block(T.s_par, c), T.a_par[:], block(T.cst, c),
-                        AluOpType.mult).then_inc(sem["scaled_par%d" % consts.index(c)], 1)
-    v.wait_ge(sem.par_done, 1)
-    v.tensor_copy(T.y_send[:], T.p_par[:, 0:TK]).then_inc(sem.rounded, 1)
-    v.wait_ge(sem.own_done, 1)
+    rules = [mix_rule(src(k), rank, prank) for k in out_mix]
+    v.wait_ge(sem.x_ld, 16)
+    for i, (f, _, _) in enumerate(rules):
+        v.tensor_scalar(T.tmp[:, i * TK:(i + 1) * TK], T.x_own[:], float(f), None,
+                        AluOpType.mult).then_inc(sem.tmp_done, 1)
+    v.wait_ge(sem.tmp_done, len(rules))
+    v.wait_ge(sem.xs_arr, n_rest)
+    for i, (_, both, _) in enumerate(rules):
+        part = T.tmp[:, i * TK:(i + 1) * TK]
+        if both:
+            op = v.tensor_tensor(mix_out[i][:], part, T.x_par[:], AluOpType.add)
+        else:
+            op = v.tensor_copy(mix_out[i][:], part)
+        op.then_inc(sem["mixed%d" % i], 1)
+    wh = TK // NH
+    for h in range(NH):
+        v.wait_ge(sem["par_done%d" % h], 1)
+        v.tensor_copy(T.y_send[:, h * wh:(h + 1) * wh], T["p_par%d" % h][:, 0:wh]).then_inc(sem.rounded, 1)
     v.wait_ge(sem.y_arr, n_rest)
-    v.tensor_tensor(T.y_out[:], T.p_own[:, 0:TK], T.y_land[:], AluOpType.add).then_inc(sem.summed, 1)
+    wb = TK // NB
+    for b in range(NB):
+        v.wait_ge(sem["own_done%d" % b], 1)
+        v.tensor_tensor(T.y_out[:, b * wb:(b + 1) * wb], T["p_own%d" % b][:, 0:wb], T.y_land[:, b * wb:(b + 1) * wb],
+                        AluOpType.add).then_inc(sem.summed, 1)
 
     t = g.tensor
     t.wait_ge(sem.x_ld, 16)
     t.wait_ge(sem.a_ld, 16)
     t.wait_ge(sem.scaled_own, len(need_own))
-    live = [n for n, (_, j, r) in enumerate(jobs) if coef[r][j] != 0]
-    seen = {rank}
-    for n, (x_ap, j, r) in enumerate(jobs):
-        if j not in seen:
-            t.wait_ge(sem["arr%d" % j], n_off)
-            seen.add(j)
-        if r == prank and "a_par" not in seen:
+    live = [n for n, job in enumerate(jobs) if job[2] != 0]
+    seen = set()
+    for n, (x_t, arrival, w, r) in enumerate(jobs):
+        if arrival is not None and arrival[0] not in seen:
+            t.wait_ge(sem[arrival[0]], arrival[1])
+            seen.add(arrival[0])
+        if r == prank and "a_arr" not in seen:
             t.wait_ge(sem.a_arr, n_rest)
-            seen.add("a_par")
+            seen.add("a_arr")
         if n not in live:
             continue
-        c = coef[r][j]
-        if r == prank and c != 1 and ("par", c) not in seen:
-            t.wait_ge(sem["scaled_par%d" % consts.index(c)], 1)
-            seen.add(("par", c))
-        raw, scaled, acc, done = ((T.a_own, T.s_own, T.p_own, sem.own_done) if r == rank
-                                  else (T.a_par, T.s_par, T.p_par, sem.par_done))
-        group = [q for q in live if jobs[q][2] == r]
-        mm = t.matmul(acc[:, 0:TK], raw[:] if c == 1 else block(scaled, c), x_ap,
-                      start=(n == group[0]), stop=(n == group[-1]))
-        if n == group[-1]:
-            mm.then_inc(done, 1)
+        if r == prank and w != 1:
+            name = "scaled_par%d" % need_par.index(w)
+            if name not in seen:
+                t.wait_ge(sem[name], 1)
+                seen.add(name)
+        raw, scaled, acc, done, nb = ((T.a_own, T.s_own, "p_own%d", "own_done%d", NB) if r == rank
+                                      else (T.a_par, T.s_par, "p_par%d", "par_done%d", NH))
+        group = [q for q in live if jobs[q][3] == r]
+        wd = TK // nb
+        for b in range(nb):
+            mm = t.matmul(T[acc % b][:, 0:wd], raw[:] if w == 1 else block(scaled, w), x_t[:, b * wd:(b + 1) * wd],
+                          start=(n == group[0]), stop=(n == group[-1]))
+            if n == group[-1]:
+                mm.then_inc(sem[done % b], 1)
 
-    g.sync.wait_ge(sem.summed, 1)
+    g.sync.wait_ge(sem.summed, NB)
     g.sync.dma_start(T.y[:], T.y_out[:]).then_inc(sem.stored, 16)
     g.sync.wait_ge(sem.stored, 16)

from concourse.bass import DstId, RemoteDMATransfer
from concourse.mybir import AluOpType, ActivationFunctionType

TK = 256
M = 128
N = 10
NCONST = 4
NRAW = 2
NB = 4
NH = 2

SCRATCH = {
    "x_own": ("sbuf", [128, TK], "bfloat16"),
    "x_par": ("sbuf", [128, TK], "bfloat16"),
    "raw0": ("sbuf", [128, TK], "bfloat16"),
    "raw1": ("sbuf", [128, TK], "bfloat16"),
    "mixin0": ("sbuf", [128, TK], "bfloat16"),
    "mixin1": ("sbuf", [128, TK], "bfloat16"),
    "mixout0": ("sbuf", [128, TK], "bfloat16"),
    "mixout1": ("sbuf", [128, TK], "bfloat16"),
    "a_own": ("sbuf", [128, M], "bfloat16"),
    "a_par": ("sbuf", [128, M], "bfloat16"),
    "s_own": ("sbuf", [128, NCONST * M], "bfloat16"),
    "s_par": ("sbuf", [128, NCONST * M], "bfloat16"),
    "y_send": ("sbuf", [128, TK], "bfloat16"),
    "y_land": ("sbuf", [128, TK], "bfloat16"),
    "y_out": ("sbuf", [128, TK], "bfloat16"),
    "tmp": ("psum", [128, 512], "float32"),
}
for _b in range(NB):
    SCRATCH["p_own%d" % _b] = ("psum", [128, 512], "float32")
for _h in range(NH):
    SCRATCH["p_par%d" % _h] = ("psum", [128, 512], "float32")

SEMAPHORES = (["x_ld", "a_ld", "scaled_own", "xs_arr", "a_arr", "tmp_done", "mixed0", "mixed1", "rounded", "y_arr",
               "summed", "stored", "sent"]
              + ["arr%d" % r for r in range(N)] + ["scaled_par%d" % i for i in range(NCONST)]
              + ["own_done%d" % b for b in range(NB)] + ["par_done%d" % h for h in range(NH)])


def _bits(mask):
    return bin(mask).count("1")


def rank_program(g, core, T, topo):
    rank = T.rank_of(core)
    if rank is None:
        return
    coef = T.tables["COEF"]
    sem = T.sem

    chips = sorted({topo.chip(c) for c in T.cores})
    nch = len(chips)
    me = chips.index(topo.chip(core))
    partner = [c for c in T.cores if c != core and topo.chip(c) == topo.chip(core)][0]
    prank = T.rank_of(partner)
    same_die = [[c for c in T.cores if topo.chip(c) == ch and topo.die(c) == topo.die(core)][0] for ch in chips]
    other_die = [[c for c in T.cores if topo.chip(c) == ch and topo.die(c) != topo.die(core)][0] for ch in chips]
    out_order = [(me + o) % nch for o in range(1, nch)]
    in_order = [(me - o) % nch for o in range(1, nch)]
    out_raw, out_mix = out_order[:NRAW], out_order[NRAW:]
    in_raw, in_mix = in_order[:NRAW], in_order[NRAW:]
    raw_land = [T.raw0, T.raw1]
    mix_land = [T.mixin0, T.mixin1]
    mix_out = [T.mixout0, T.mixout1]

    off_mask = topo.mask(core, same_die[out_order[0]])
    rest_mask = topo.mask(core, partner) & ~off_mask
    n_off, n_rest = _bits(off_mask), _bits(rest_mask)

    def mix_rule(r, s_me, s_par):
        cm, cp = coef[r][s_me], coef[r][s_par]
        if cp != 0:
            return cm / cp, True, cp
        return 1.0, False, cm

    def src(k):
        return T.rank_of(same_die[k])

    def arr(k):
        return ("arr%d" % src(k), n_off)

    jobs = [(T.x_own, None, coef[rank][rank], rank),
            (T.x_par, ("xs_arr", n_rest), coef[rank][prank], rank),
            (raw_land[0], arr(in_raw[0]), coef[rank][src(in_raw[0])], rank)]
    jobs += [(raw_land[i], arr(k), coef[prank][src(k)], prank) for i, k in enumerate(in_raw)]
    jobs += [(raw_land[i], arr(k), coef[rank][src(k)], rank) for i, k in enumerate(in_raw) if i > 0]
    jobs += [(mix_land[i], arr(k), mix_rule(rank, src(k), T.rank_of(other_die[k]))[2], rank)
             for i, k in enumerate(in_mix)]

    consts = sorted({c for row in coef for c in row} - {0, 1})
    need_own, need_par = [], []
    for _, _, w, r in jobs:
        lst = need_own if r == rank else need_par
        if w in consts and w not in lst:
            lst.append(w)

    def block(t, c):
        i = consts.index(c)
        return t[:, i * M:(i + 1) * M]

    g.sync.dma_start(T.x_own[:], T.x[:]).then_inc(sem.x_ld, 16)
    g.scalar.dma_start(T.a_own[:], T.a[:]).then_inc(sem.a_ld, 16)

    my_arr = sem["arr%d" % rank]
    prid, ppid, _ = topo.addr(partner)
    g.wait_ge(sem.x_ld, 16)
    ids = []
    for k in out_raw:
        rid, pid, _ = topo.addr(same_die[k])
        ids.append(DstId(rid=rid, pnc=pid))
    g.remote_dma_fused(
        [RemoteDMATransfer(dst_ids=ids, dma_engine_mask=off_mask, remote_sem=my_arr,
                           srcs=[T.x_own[:]], dsts=[raw_land[i][:] for i in range(len(out_raw))], alu_op=0)],
        local_sem=sem.sent)
    g.remote_dma(out_ap=T.x_par[:], in_ap=T.x_own[:], remote_sem=sem.xs_arr, local_sem=sem.sent,
                 pid=ppid, routing_id=prid, dma_engine_mask=rest_mask)
    g.wait_ge(sem.a_ld, 16)
    g.remote_dma(out_ap=T.a_par[:], in_ap=T.a_own[:], remote_sem=sem.a_arr, local_sem=sem.sent,
                 pid=ppid, routing_id=prid, dma_engine_mask=rest_mask)
    for i, k in enumerate(out_mix):
        rid, pid, _ = topo.addr(same_die[k])
        g.wait_ge(sem["mixed%d" % i], 1)
        g.remote_dma(out_ap=mix_land[i][:], in_ap=mix_out[i][:], remote_sem=my_arr, local_sem=sem.sent,
                     pid=pid, routing_id=rid, dma_engine_mask=off_mask)
    g.wait_ge(sem.rounded, NH)
    g.remote_dma(out_ap=T.y_land[:], in_ap=T.y_send[:], remote_sem=sem.y_arr, local_sem=sem.sent,
                 pid=ppid, routing_id=prid, dma_engine_mask=rest_mask)
    g.wait_ge(sem.sent, n_off * (1 + len(out_mix)) + 3 * n_rest)

    sc = g.scalar
    sc.wait_ge(sem.a_ld, 16)
    for c in need_own:
        sc.activation(block(T.s_own, c), T.a_own[:], ActivationFunctionType.Copy,
                      scale=float(c)).then_inc(sem.scaled_own, 1)
    sc.wait_ge(sem.a_arr, n_rest)
    for i, c in enumerate(need_par):
        sc.activation(block(T.s_par, c), T.a_par[:], ActivationFunctionType.Copy,
                      scale=float(c)).then_inc(sem["scaled_par%d" % i], 1)

    v = g.vector
    rules = [mix_rule(src(k), rank, prank) for k in out_mix]
    v.wait_ge(sem.x_ld, 16)
    for i, (f, _, _) in enumerate(rules):
        v.tensor_scalar(T.tmp[:, i * TK:(i + 1) * TK], T.x_own[:], float(f), None,
                        AluOpType.mult).then_inc(sem.tmp_done, 1)
    v.wait_ge(sem.tmp_done, len(rules))
    v.wait_ge(sem.xs_arr, n_rest)
    for i, (_, both, _) in enumerate(rules):
        part = T.tmp[:, i * TK:(i + 1) * TK]
        if both:
            op = v.tensor_tensor(mix_out[i][:], part, T.x_par[:], AluOpType.add)
        else:
            op = v.tensor_copy(mix_out[i][:], part)
        op.then_inc(sem["mixed%d" % i], 1)
    wh = TK // NH
    for h in range(NH):
        v.wait_ge(sem["par_done%d" % h], 1)
        v.tensor_copy(T.y_send[:, h * wh:(h + 1) * wh], T["p_par%d" % h][:, 0:wh]).then_inc(sem.rounded, 1)
    v.wait_ge(sem.y_arr, n_rest)
    wb = TK // NB
    for b in range(NB):
        v.wait_ge(sem["own_done%d" % b], 1)
        v.tensor_tensor(T.y_out[:, b * wb:(b + 1) * wb], T["p_own%d" % b][:, 0:wb], T.y_land[:, b * wb:(b + 1) * wb],
                        AluOpType.add).then_inc(sem.summed, 1)

    t = g.tensor
    t.wait_ge(sem.x_ld, 16)
    t.wait_ge(sem.a_ld, 16)
    t.wait_ge(sem.scaled_own, len(need_own))
    live = [n for n, job in enumerate(jobs) if job[2] != 0]
    seen = set()
    for n, (x_t, arrival, w, r) in enumerate(jobs):
        if arrival is not None and arrival[0] not in seen:
            t.wait_ge(sem[arrival[0]], arrival[1])
            seen.add(arrival[0])
        if r == prank and "a_arr" not in seen:
            t.wait_ge(sem.a_arr, n_rest)
            seen.add("a_arr")
        if n not in live:
            continue
        if r == prank and w != 1:
            name = "scaled_par%d" % need_par.index(w)
            if name not in seen:
                t.wait_ge(sem[name], 1)
                seen.add(name)
        raw, scaled, acc, done, nb = ((T.a_own, T.s_own, "p_own%d", "own_done%d", NB) if r == rank
                                      else (T.a_par, T.s_par, "p_par%d", "par_done%d", NH))
        group = [q for q in live if jobs[q][3] == r]
        wd = TK // nb
        for b in range(nb):
            mm = t.matmul(T[acc % b][:, 0:wd], raw[:] if w == 1 else block(scaled, w), x_t[:, b * wd:(b + 1) * wd],
                          start=(n == group[0]), stop=(n == group[-1]))
            if n == group[-1]:
                mm.then_inc(sem[done % b], 1)

    g.sync.wait_ge(sem.summed, NB)
    g.sync.dma_start(T.y[:], T.y_out[:]).then_inc(sem.stored, 16)
    g.sync.wait_ge(sem.stored, 16)
